import numpy as np
import ml_dtypes


def mxq(x, axis, fmt="e4m3"):
    dtype, down = {"e4m3": (ml_dtypes.float8_e4m3fn, 7), "e5m2": (ml_dtypes.float8_e5m2, 14)}[fmt]
    v = np.moveaxis(np.asarray(x, np.float32).astype(ml_dtypes.bfloat16).astype(np.float64), axis, -1)
    blocks = v.reshape(v.shape[:-1] + (-1, 32))
    amax = np.abs(blocks).max(-1, keepdims=True)
    byte = np.maximum(np.where(amax > 0, np.frexp(amax)[1] - 1 + 127, 0) - down, 1)
    scale = np.exp2(byte - 127.0)
    codes = (blocks / scale).astype(np.float32).astype(dtype).astype(np.float64)
    return np.moveaxis((codes * scale).reshape(v.shape), -1, axis)


WIDE = False


def mx_kscale(k):
    if not WIDE:
        return np.ones(k)
    levels = np.array([10, -10, 5, -5, 0])
    if k % 512:
        return np.exp2(np.random.permutation(np.resize(levels, k // 32))).repeat(32)
    a = np.empty((k // 512, 16))
    for p in range(k // 512):
        a[p, :8] = np.random.permutation(np.resize(levels, 8))
        for g in range(8):
            far = levels[np.abs(levels - a[p, g]) >= 10]
            a[p, g + 8] = far[np.random.randint(len(far))]
    return np.exp2(a.ravel()).repeat(32)


BF16 = ml_dtypes.bfloat16


def bf(x):
    return np.asarray(x, np.float32).astype(BF16)


def f64(x):
    return np.asarray(x).astype(np.float64)


E2M1 = np.array([0.0, 0.5, 1.0, 1.5, 2.0, 3.0, 4.0, 6.0, -0.0, -0.5, -1.0, -1.5, -2.0, -3.0, -4.0, -6.0])


def pack_weight(w, fmt):
    k, n = w.shape
    w = f64(bf(w)).reshape(k // 32, 32, n)
    amax = np.abs(w).max(1)
    if fmt == "e4m3":
        byte = np.frexp(amax)[1] - 1 + 127 - 7
    else:
        mant, ex = np.frexp(amax / 6.0)
        byte = np.where(mant > 0.5, ex, ex - 1) + 127
    byte = np.clip(np.where(amax > 0, byte, 1), 1, 254)
    scaled = (w * np.exp2(127.0 - byte)[:, None, :]).reshape(k, n).astype(np.float32)
    by_word = np.ascontiguousarray(scaled.reshape(k // 512, 128, 4, n).transpose(0, 1, 3, 2))
    if fmt == "e4m3":
        words = by_word.astype(ml_dtypes.float8_e4m3fn).view(np.uint8)
    else:
        c = by_word.astype(ml_dtypes.float4_e2m1fn).view(np.uint8) & 0xF
        words = c[..., 0::2] | (c[..., 1::2] << 4)
    return np.ascontiguousarray(words), np.ascontiguousarray(byte.astype(np.uint8).reshape(k // 512, 16, n))


def unpack_weight(words, scales, fmt):
    g, p, n, _ = words.shape
    if fmt == "e4m3":
        vals = np.ascontiguousarray(words).view(ml_dtypes.float8_e4m3fn).astype(np.float64)
    else:
        nib = np.empty((g, p, n, 4), np.uint8)
        nib[..., 0::2] = words & 0xF
        nib[..., 1::2] = words >> 4
        vals = E2M1[nib]
    vals = vals * np.repeat(np.exp2(scales.astype(np.float64) - 127.0), 8, axis=1)[..., None]
    return vals.transpose(0, 1, 3, 2).reshape(g * 512, n)
def pack4(w):
    words, scales = pack_weight(w, "e2m1")
    return words.reshape(words.shape[0], 128, -1), scales


def unpack4(words, scales):
    return unpack_weight(words.reshape(words.shape[0], 128, -1, 2), scales, "e2m1")


def planes(Y):
    n, m = Y.shape
    b = f64(bf(Y)).reshape(n // 32, 32, m)
    amax = np.abs(b).max(1)
    byte = np.clip(np.where(amax > 0, np.frexp(amax)[1] - 1 + 127 - 7, 1), 1, 254)
    codes = (b * np.exp2(127.0 - byte)[:, None, :]).reshape(n, m).astype(np.float32).astype(ml_dtypes.float8_e4m3fn).view(np.uint8)
    words = codes.reshape(n // 512, 128, 4, m).transpose(0, 1, 3, 2)
    return np.ascontiguousarray(words), np.ascontiguousarray(byte.astype(np.uint8).reshape(n // 512, 16, m))


M, K, N = 2048, 1024, 1024

def noise(*shape):
    return np.random.standard_normal(shape)

def setup_inputs():
    s = mx_kscale(K)
    x = noise(K, M) * s[:, None]
    x_words, x_scales = pack_weight(x, "e4m3")
    w = noise(K, N) / np.sqrt(K) / s[:, None]
    b = 0.3 * noise(N)
    gain = np.exp(0.8 * noise(N))
    return {"x_words": x_words, "x_scales": x_scales,
            "w": bf(w), "b": bf(b), "gain": bf(gain)}

def reference(x_words, x_scales, w, b, gain):
    x = unpack_weight(x_words, x_scales, "e4m3")
    wq = mxq(f64(w), 0, "e4m3")
    z = (x.T @ wq) + f64(b)
    y = np.tanh(z) * f64(gain)
    Y = y.T
    words, scales = planes(Y)
    return y, words, scales

@@ -1,0 +1,248 @@
+from contextlib import ExitStack
+
+import concourse.mybir as mybir
+from concourse.masks import make_identity
+
+M, K, N = 2048, 1024, 1024
+FLOPS = 2 * M * K * N
+
+F32 = mybir.dt.float32
+BF16 = mybir.dt.bfloat16
+I32 = mybir.dt.int32
+U32 = mybir.dt.uint32
+U8 = mybir.dt.uint8
+FP8X4 = mybir.dt.float8_e4m3fn_x4
+ACT = mybir.ActivationFunctionType
+ALU = mybir.AluOpType
+
+P = 128
+PACK = 4
+GROUP = P * PACK
+PASSES = K // GROUP
+GROUPS = N // GROUP
+CHUNK = 512
+CHUNKS = M // CHUNK
+STEPS = GROUPS * CHUNKS
+BLOCKS = CHUNK // P
+
+
+def tile_scaled_tanh_pooler_g6_kernel(tc, x_words, x_scales, w, b, gain, out_0, out_1, out_2):
+    nc = tc.nc
+    with ExitStack() as ctx:
+        keep = ctx.enter_context(tc.tile_pool(name="keep", bufs=1))
+        work = ctx.enter_context(tc.tile_pool(name="work", bufs=3))
+        outs = ctx.enter_context(tc.tile_pool(name="outs", bufs=8))
+        psum = ctx.enter_context(tc.psum_pool(name="psum", bufs=1))
+        ctx.enter_context(tc.manual_schedule())
+
+        bias = keep.tile([P, GROUPS, PACK], BF16, name="bias")
+        gains = keep.tile([P, GROUPS, PACK], BF16, name="gains")
+        nc.gpsimd.dma_start(out=bias[:], in_=b.rearrange("(g p t) -> p g t", p=P, t=PACK))
+        nc.gpsimd.dma_start(out=gains[:], in_=gain.rearrange("(g p t) -> p g t", p=P, t=PACK))
+        ident = keep.tile([P, P], F32, name="ident")
+        make_identity(nc, ident[:])
+
+        xs_first = keep.tile([P, CHUNK], U8, name="xs_first", align_bytes=64)
+        xs_rest = keep.tile([P, M - CHUNK], U8, name="xs_rest", align_bytes=64)
+        warm = keep.tile([P, 8], F32, name="warm")
+        warm_out = keep.tile([P, 8], F32, name="warm_out")
+        nc.vector.memset(xs_first[:].bitcast(I32), 0)
+        nc.vector.memset(warm[:], 0.0)
+        nc.vector.memset(xs_rest[:].bitcast(I32), 0)
+        nc.scalar.activation(out=warm_out[:], in_=warm[:], func=ACT.Tanh)
+
+        w_raw = {}
+        x_codes = {}
+
+        def load_w(k, g):
+            raw = keep.tile([P, PACK, GROUP], BF16, name="w_raw_%d_%d" % (k, g))
+            rows = w[k * GROUP:(k + 1) * GROUP, g * GROUP:(g + 1) * GROUP]
+            nc.sync.dma_start(out=raw[:], in_=rows.rearrange("(p j) c -> p j c", j=PACK))
+            w_raw[k, g] = raw
+
+        def load_x(c, ks):
+            codes = keep.tile([P, len(ks), CHUNK], U32, name="x_%d_%d" % (c, ks[0]), align_bytes=64)
+            src = x_words.rearrange("k p n t -> p k (n t)")
+            src = src[:, ks[0]:ks[-1] + 1, c * CHUNK * PACK:(c + 1) * CHUNK * PACK]
+            nc.sync.dma_start(out=codes[:].bitcast(I32), in_=src.bitcast(I32))
+            for i, k in enumerate(ks):
+                x_codes[c, k] = codes[:, i, :]
+
+        def load_x_scales(plane, n0, n1):
+            for q in range(4):
+                nc.sync.dma_start(
+                    out=plane[32 * q:32 * q + 4 * PASSES, :].bitcast(I32),
+                    in_=x_scales[:, 4 * q:4 * q + 4, n0:n1].bitcast(I32),
+                )
+
+        def x_plane(c, k):
+            if c == 0:
+                return xs_first[4 * k:P, :]
+            return xs_rest[4 * k:P, (c - 1) * CHUNK:c * CHUNK]
+
+        load_w(0, 0)
+        load_x(0, [0])
+        load_x_scales(xs_first, 0, CHUNK)
+        load_w(1, 0)
+        load_x(0, [1])
+        load_x(1, [0, 1])
+        load_x_scales(xs_rest, CHUNK, M)
+        load_w(0, 1)
+        load_w(1, 1)
+        load_x(2, [0, 1])
+        load_x(3, [0, 1])
+
+        w_grouped = {}
+        w_codes = {}
+        w_scales = {}
+
+        def interleave_w(k, g, t, on_scalar):
+            grouped = keep.tile([P, P, PACK], BF16, name="w_grouped_%d_%d_%d" % (k, g, t), align_bytes=64)
+            src = w_raw[k, g][:].rearrange("p j (m t) -> p t m j", t=PACK)[:, t, :, :]
+            if on_scalar:
+                nc.scalar.copy(out=grouped[:], in_=src)
+            else:
+                nc.vector.tensor_copy(out=grouped[:], in_=src)
+            w_grouped[k, g, t] = grouped
+
+        def quantize_w(k, g, t):
+            codes = keep.tile([P, P], U32, name="w_codes_%d_%d_%d" % (k, g, t), align_bytes=64)
+            scales = keep.tile([P, P], U8, name="w_scales_%d_%d_%d" % (k, g, t), align_bytes=64)
+            nc.vector.quantize_mx(
+                out=codes[:].bitcast(FP8X4),
+                scales=scales[:],
+                in_=w_grouped[k, g, t][:].rearrange("p m j -> p (m j)"),
+            )
+            w_codes[k, g, t] = codes
+            w_scales[k, g, t] = scales
+
+        acc = {}
+        tanh_t = {}
+        y_t = {}
+        y_packed = {}
+        turned = {}
+        y_scales = [keep.tile([P, M], U8, name="y_scales_%d" % g, align_bytes=64) for g in range(GROUPS)]
+
+        def mx_pass(s, t, k):
+            g, c = divmod(s, CHUNKS)
+            if k == 0:
+                acc[s, t] = psum.tile([P, CHUNK], F32, name="acc_%d" % t)
+            nc.tensor.matmul_mx(
+                out=acc[s, t][:],
+                lhsT=w_codes[k, g, t][:].bitcast(FP8X4),
+                lhsT_scale=w_scales[k, g, t][:],
+                rhs=x_codes[c, k].bitcast(FP8X4),
+                rhs_scale=x_plane(c, k),
+                start=(k == 0),
+                stop=(k == PASSES - 1),
+            )
+
+        def multiply(s):
+            for t in range(PACK):
+                for k in range(PASSES):
+                    mx_pass(s, t, k)
+
+        def tanh(s, t):
+            g = s // CHUNKS
+            if t == 0:
+                tanh_t[s] = work.tile([P, PACK, CHUNK], F32, name="tanh_t")
+            nc.scalar.activation(out=tanh_t[s][:, t, :], in_=acc[s, t][:], func=ACT.Tanh, bias=bias[:, g, t:t + 1])
+
+        def scale(s, t):
+            g = s // CHUNKS
+            if t == 0:
+                y_t[s] = work.tile([P, PACK, CHUNK], F32, name="y_t")
+            nc.vector.tensor_scalar(
+                out=y_t[s][:, t, :], in0=tanh_t[s][:, t, :], scalar1=gains[:, g, t:t + 1], scalar2=None, op0=ALU.mult
+            )
+
+        def interleave_y(s):
+            y_packed[s] = work.tile([P, CHUNK, PACK], BF16, name="y_packed", align_bytes=64)
+            nc.vector.tensor_copy(
+                out=y_packed[s][:].rearrange("p (c i) t -> p c t i", i=4),
+                in_=y_t[s][:].rearrange("p t (c i) -> p c t i", i=4),
+            )
+
+        def quantize_y(s):
+            g, c = divmod(s, CHUNKS)
+            codes = work.tile([P, CHUNK], U32, name="y_codes", align_bytes=64)
+            nc.vector.quantize_mx(
+                out=codes[:].bitcast(FP8X4),
+                scales=y_scales[g][:, c * CHUNK:(c + 1) * CHUNK],
+                in_=y_packed[s][:].rearrange("p n t -> p (n t)"),
+            )
+            dst = out_1[g].rearrange("p n t -> p (n t)")[:, c * CHUNK * PACK:(c + 1) * CHUNK * PACK]
+            nc.sync.dma_start(out=dst.bitcast(I32), in_=codes[:].bitcast(I32))
+            if c == CHUNKS - 1:
+                for q in range(4):
+                    nc.sync.dma_start(
+                        out=out_2[g, 4 * q:4 * q + 4, :].bitcast(I32),
+                        in_=y_scales[g][32 * q:32 * q + 4, :].bitcast(I32),
+                    )
+
+        def transpose(s):
+            for j in range(BLOCKS):
+                turned[s, j] = psum.tile([P, PACK, P], F32, name="turned_%d" % j)
+                for t in range(PACK):
+                    nc.tensor.transpose(turned[s, j][:, t, :], y_t[s][:, t, j * P:(j + 1) * P], ident[:])
+
+        def emit(s, j, on_scalar):
+            g, c = divmod(s, CHUNKS)
+            rows = outs.tile([P, P, PACK], F32, name="rows")
+            src = turned[s, j][:].rearrange("n t m -> n m t")
+            if on_scalar:
+                nc.scalar.copy(out=rows[:], in_=src)
+            else:
+                nc.vector.tensor_copy(out=rows[:], in_=src)
+            n0 = c * CHUNK + j * P
+            nc.sync.dma_start(
+                out=out_0[n0:n0 + P, g * GROUP:(g + 1) * GROUP], in_=rows[:].rearrange("n m t -> n (m t)")
+            )
+
+        for k in range(PASSES):
+            for t in range(PACK):
+                interleave_w(k, 0, t, on_scalar=(t >= 2))
+            for t in range(PACK):
+                quantize_w(k, 0, t)
+            for t in range(PACK):
+                mx_pass(0, t, k)
+
+        later = [(k, 1, t) for k in range(PASSES) for t in range(PACK)]
+        shares = {-1: later[0:2], 0: later[2:5], 1: later[5:8]}
+
+        def prepare(pieces):
+            for piece in pieces:
+                interleave_w(*piece, on_scalar=False)
+            for piece in pieces:
+                quantize_w(*piece)
+
+        for t in range(PACK):
+            tanh(0, t)
+            scale(0, t)
+        prepare(shares[-1])
+        multiply(1)
+
+        for s in range(STEPS):
+            more = s + 1 < STEPS
+            transpose(s)
+            if more:
+                interleave_y(s)
+                for t in (0, 1):
+                    tanh(s + 1, t)
+                    scale(s + 1, t)
+                quantize_y(s)
+                for t in (2, 3):
+                    tanh(s + 1, t)
+                    scale(s + 1, t)
+                prepare(shares.get(s, []))
+                if s + 2 < STEPS:
+                    multiply(s + 2)
+                for j in range(BLOCKS):
+                    emit(s, j, on_scalar=(j < BLOCKS - 1 or s in shares))
+            else:
+                interleave_y(s)
+                emit(s, 0, on_scalar=True)
+                emit(s, 1, on_scalar=True)
+                quantize_y(s)
+                emit(s, 2, on_scalar=True)
+                emit(s, 3, on_scalar=False)

@@ -30,15 +30,12 @@ def tile_scaled_tanh_pooler_g6_kernel(tc, x_words, x_scales, w, b, gain, out_0, 
     nc = tc.nc
     with ExitStack() as ctx:
         keep = ctx.enter_context(tc.tile_pool(name="keep", bufs=1))
-        work = ctx.enter_context(tc.tile_pool(name="work", bufs=3))
-        outs = ctx.enter_context(tc.tile_pool(name="outs", bufs=8))
+        work = ctx.enter_context(tc.tile_pool(name="work", bufs=2))
         psum = ctx.enter_context(tc.psum_pool(name="psum", bufs=1))
         ctx.enter_context(tc.manual_schedule())
 
         bias = keep.tile([P, GROUPS, PACK], BF16, name="bias")
         gains = keep.tile([P, GROUPS, PACK], BF16, name="gains")
-        nc.gpsimd.dma_start(out=bias[:], in_=b.rearrange("(g p t) -> p g t", p=P, t=PACK))
-        nc.gpsimd.dma_start(out=gains[:], in_=gain.rearrange("(g p t) -> p g t", p=P, t=PACK))
         ident = keep.tile([P, P], F32, name="ident")
         make_identity(nc, ident[:])
 
@@ -84,7 +81,9 @@ def tile_scaled_tanh_pooler_g6_kernel(tc, x_words, x_scales, w, b, gain, out_0, 
         load_x(0, [0])
         load_x_scales(xs_first, 0, CHUNK)
         load_w(1, 0)
+        nc.sync.dma_start(out=bias[:], in_=b.rearrange("(g p t) -> p g t", p=P, t=PACK))
         load_x(0, [1])
+        nc.sync.dma_start(out=gains[:], in_=gain.rearrange("(g p t) -> p g t", p=P, t=PACK))
         load_x(1, [0, 1])
         load_x_scales(xs_rest, CHUNK, M)
         load_w(0, 1)
@@ -96,30 +95,32 @@ def tile_scaled_tanh_pooler_g6_kernel(tc, x_words, x_scales, w, b, gain, out_0, 
         w_codes = {}
         w_scales = {}
 
-        def interleave_w(k, g, t, on_scalar):
-            grouped = keep.tile([P, P, PACK], BF16, name="w_grouped_%d_%d_%d" % (k, g, t), align_bytes=64)
-            src = w_raw[k, g][:].rearrange("p j (m t) -> p t m j", t=PACK)[:, t, :, :]
+        def interleave_w(k, g, h, on_scalar):
+            grouped = keep.tile([P, 2, P, PACK], BF16, name="w_grouped_%d_%d_%d" % (k, g, h), align_bytes=64)
+            src = w_raw[k, g][:].rearrange("p j (a m h u) -> p h a j m u", m=2, h=2, u=2)[:, h]
+            dst = grouped[:].rearrange("p u (a m) j -> p a j m u", m=2)
             if on_scalar:
-                nc.scalar.copy(out=grouped[:], in_=src)
+                nc.scalar.copy(out=dst, in_=src)
             else:
-                nc.vector.tensor_copy(out=grouped[:], in_=src)
-            w_grouped[k, g, t] = grouped
+                nc.vector.tensor_copy(out=dst, in_=src)
+            w_grouped[k, g, h] = grouped
 
-        def quantize_w(k, g, t):
-            codes = keep.tile([P, P], U32, name="w_codes_%d_%d_%d" % (k, g, t), align_bytes=64)
-            scales = keep.tile([P, P], U8, name="w_scales_%d_%d_%d" % (k, g, t), align_bytes=64)
+        def quantize_w(k, g, h):
+            codes = keep.tile([P, 2 * P], U32, name="w_codes_%d_%d_%d" % (k, g, h), align_bytes=64)
+            scales = keep.tile([P, 2 * P], U8, name="w_scales_%d_%d_%d" % (k, g, h), align_bytes=64)
             nc.vector.quantize_mx(
                 out=codes[:].bitcast(FP8X4),
                 scales=scales[:],
-                in_=w_grouped[k, g, t][:].rearrange("p m j -> p (m j)"),
+                in_=w_grouped[k, g, h][:].rearrange("p u m j -> p (u m j)"),
             )
-            w_codes[k, g, t] = codes
-            w_scales[k, g, t] = scales
+            for u in range(2):
+                w_codes[k, g, 2 * h + u] = codes[:, u * P:(u + 1) * P]
+                w_scales[k, g, 2 * h + u] = scales[:, u * P:(u + 1) * P]
 
         acc = {}
-        tanh_t = {}
-        y_t = {}
+        y_t = [keep.tile([P, PACK, CHUNK], F32, name="y_t_%d" % s) for s in range(STEPS)]
         y_packed = {}
+        y_codes = {}
         turned = {}
         y_scales = [keep.tile([P, M], U8, name="y_scales_%d" % g, align_bytes=64) for g in range(GROUPS)]
 
@@ -129,50 +130,50 @@ def tile_scaled_tanh_pooler_g6_kernel(tc, x_words, x_scales, w, b, gain, out_0, 
                 acc[s, t] = psum.tile([P, CHUNK], F32, name="acc_%d" % t)
             nc.tensor.matmul_mx(
                 out=acc[s, t][:],
-                lhsT=w_codes[k, g, t][:].bitcast(FP8X4),
-                lhsT_scale=w_scales[k, g, t][:],
+                lhsT=w_codes[k, g, t].bitcast(FP8X4),
+                lhsT_scale=w_scales[k, g, t],
                 rhs=x_codes[c, k].bitcast(FP8X4),
                 rhs_scale=x_plane(c, k),
                 start=(k == 0),
                 stop=(k == PASSES - 1),
             )
 
-        def multiply(s):
-            for t in range(PACK):
+        def multiply(s, slots):
+            for t in slots:
                 for k in range(PASSES):
                     mx_pass(s, t, k)
 
         def tanh(s, t):
             g = s // CHUNKS
-            if t == 0:
-                tanh_t[s] = work.tile([P, PACK, CHUNK], F32, name="tanh_t")
-            nc.scalar.activation(out=tanh_t[s][:, t, :], in_=acc[s, t][:], func=ACT.Tanh, bias=bias[:, g, t:t + 1])
+            nc.scalar.activation(out=y_t[s][:, t, :], in_=acc[s, t][:], func=ACT.Tanh, bias=bias[:, g, t:t + 1])
 
         def scale(s, t):
             g = s // CHUNKS
-            if t == 0:
-                y_t[s] = work.tile([P, PACK, CHUNK], F32, name="y_t")
             nc.vector.tensor_scalar(
-                out=y_t[s][:, t, :], in0=tanh_t[s][:, t, :], scalar1=gains[:, g, t:t + 1], scalar2=None, op0=ALU.mult
+                out=y_t[s][:, t, :], in0=y_t[s][:, t, :], scalar1=gains[:, g, t:t + 1], scalar2=None, op0=ALU.mult
             )
 
         def interleave_y(s):
             y_packed[s] = work.tile([P, CHUNK, PACK], BF16, name="y_packed", align_bytes=64)
             nc.vector.tensor_copy(
-                out=y_packed[s][:].rearrange("p (c i) t -> p c t i", i=4),
-                in_=y_t[s][:].rearrange("p t (c i) -> p c t i", i=4),
+                out=y_packed[s][:].rearrange("p (c i) t -> p c t i", i=2),
+                in_=y_t[s][:].rearrange("p t (c i) -> p c t i", i=2),
             )
 
         def quantize_y(s):
             g, c = divmod(s, CHUNKS)
-            codes = work.tile([P, CHUNK], U32, name="y_codes", align_bytes=64)
+            codes = keep.tile([P, CHUNK], U32, name="y_codes_%d" % s, align_bytes=64)
             nc.vector.quantize_mx(
                 out=codes[:].bitcast(FP8X4),
                 scales=y_scales[g][:, c * CHUNK:(c + 1) * CHUNK],
                 in_=y_packed[s][:].rearrange("p n t -> p (n t)"),
             )
+            y_codes[s] = codes
+
+        def store_planes(s):
+            g, c = divmod(s, CHUNKS)
             dst = out_1[g].rearrange("p n t -> p (n t)")[:, c * CHUNK * PACK:(c + 1) * CHUNK * PACK]
-            nc.sync.dma_start(out=dst.bitcast(I32), in_=codes[:].bitcast(I32))
+            nc.sync.dma_start(out=dst.bitcast(I32), in_=y_codes[s][:].bitcast(I32))
             if c == CHUNKS - 1:
                 for q in range(4):
                     nc.sync.dma_start(
@@ -180,15 +181,15 @@ def tile_scaled_tanh_pooler_g6_kernel(tc, x_words, x_scales, w, b, gain, out_0, 
                         in_=y_scales[g][32 * q:32 * q + 4, :].bitcast(I32),
                     )
 
-        def transpose(s):
-            for j in range(BLOCKS):
+        def transpose(s, blocks):
+            for j in blocks:
                 turned[s, j] = psum.tile([P, PACK, P], F32, name="turned_%d" % j)
                 for t in range(PACK):
                     nc.tensor.transpose(turned[s, j][:, t, :], y_t[s][:, t, j * P:(j + 1) * P], ident[:])
 
         def emit(s, j, on_scalar):
             g, c = divmod(s, CHUNKS)
-            rows = outs.tile([P, P, PACK], F32, name="rows")
+            rows = keep.tile([P, P, PACK], F32, name="rows_%d_%d" % (s, j))
             src = turned[s, j][:].rearrange("n t m -> n m t")
             if on_scalar:
                 nc.scalar.copy(out=rows[:], in_=src)
@@ -199,50 +200,62 @@ def tile_scaled_tanh_pooler_g6_kernel(tc, x_words, x_scales, w, b, gain, out_0, 
                 out=out_0[n0:n0 + P, g * GROUP:(g + 1) * GROUP], in_=rows[:].rearrange("n m t -> n (m t)")
             )
 
+        def last_first(order):
+            return order[-1:] + order[:-1]
+
         for k in range(PASSES):
-            for t in range(PACK):
-                interleave_w(k, 0, t, on_scalar=(t >= 2))
-            for t in range(PACK):
-                quantize_w(k, 0, t)
+            interleave_w(k, 0, 0, on_scalar=False)
+            interleave_w(k, 0, 1, on_scalar=True)
+            for h in range(2):
+                quantize_w(k, 0, h)
             for t in range(PACK):
                 mx_pass(0, t, k)
 
-        later = [(k, 1, t) for k in range(PASSES) for t in range(PACK)]
-        shares = {-1: later[0:2], 0: later[2:5], 1: later[5:8]}
+        later = [(k, 1, h) for k in range(PASSES) for h in range(2)]
 
-        def prepare(pieces):
-            for piece in pieces:
-                interleave_w(*piece, on_scalar=False)
-            for piece in pieces:
-                quantize_w(*piece)
-
-        for t in range(PACK):
+        slots = list(range(PACK))
+        for t in slots:
             tanh(0, t)
+            if t == slots[-1]:
+                interleave_w(*later[0], on_scalar=False)
             scale(0, t)
-        prepare(shares[-1])
-        multiply(1)
+        quantize_w(*later[0])
+        multiply(1, slots)
 
-        for s in range(STEPS):
-            more = s + 1 < STEPS
-            transpose(s)
-            if more:
+        blocks = list(range(BLOCKS))
+        for s in range(STEPS - 1):
+            piece = later[s + 1] if s + 1 < len(later) else None
+            transpose(s, blocks)
+            if piece:
+                interleave_w(*piece, on_scalar=False)
                 interleave_y(s)
-                for t in (0, 1):
-                    tanh(s + 1, t)
-                    scale(s + 1, t)
-                quantize_y(s)
-                for t in (2, 3):
-                    tanh(s + 1, t)
-                    scale(s + 1, t)
-                prepare(shares.get(s, []))
-                if s + 2 < STEPS:
-                    multiply(s + 2)
-                for j in range(BLOCKS):
-                    emit(s, j, on_scalar=(j < BLOCKS - 1 or s in shares))
+                quantize_w(*piece)
+                on_vector = []
             else:
                 interleave_y(s)
-                emit(s, 0, on_scalar=True)
-                emit(s, 1, on_scalar=True)
-                quantize_y(s)
-                emit(s, 2, on_scalar=True)
-                emit(s, 3, on_scalar=False)
+                on_vector = blocks[:1]
+                emit(s, blocks[0], on_scalar=False)
+            if s > 0:
+                slots = last_first(slots)
+            for t in slots:
+                tanh(s + 1, t)
+            for t in (last_first(slots) if s + 2 < STEPS else slots):
+                scale(s + 1, t)
+            quantize_y(s)
+            if s + 2 < STEPS:
+                multiply(s + 2, slots)
+            on_scalar = last_first(blocks[len(on_vector):])
+            for j in on_scalar:
+                emit(s, j, on_scalar=True)
+            store_planes(s)
+            blocks = on_vector + on_scalar
+
+        s = STEPS - 1
+        transpose(s, blocks)
+        interleave_y(s)
+        emit(s, blocks[0], on_scalar=True)
+        emit(s, blocks[1], on_scalar=True)
+        emit(s, blocks[2], on_scalar=True)
+        quantize_y(s)
+        emit(s, blocks[3], on_scalar=True)
+        store_planes(s)

@@ -24,6 +24,8 @@ CHUNK = 512
 CHUNKS = M // CHUNK
 STEPS = GROUPS * CHUNKS
 BLOCKS = CHUNK // P
+WHOLE = (0, CHUNK)
+HALVES = ((0, CHUNK // 2), (CHUNK // 2, CHUNK))
 
 
 def tile_scaled_tanh_pooler_g6_kernel(tc, x_words, x_scales, w, b, gain, out_0, out_1, out_2):
@@ -39,8 +41,8 @@ def tile_scaled_tanh_pooler_g6_kernel(tc, x_words, x_scales, w, b, gain, out_0, 
         ident = keep.tile([P, P], F32, name="ident")
         make_identity(nc, ident[:])
 
-        xs_first = keep.tile([P, CHUNK], U8, name="xs_first", align_bytes=64)
-        xs_rest = keep.tile([P, M - CHUNK], U8, name="xs_rest", align_bytes=64)
+        xs_first = keep.tile([P, M // 2], U8, name="xs_first", align_bytes=64)
+        xs_rest = keep.tile([P, M // 2], U8, name="xs_rest", align_bytes=64)
         warm = keep.tile([P, 8], F32, name="warm")
         warm_out = keep.tile([P, 8], F32, name="warm_out")
         nc.vector.memset(xs_first[:].bitcast(I32), 0)
@@ -57,13 +59,19 @@ def tile_scaled_tanh_pooler_g6_kernel(tc, x_words, x_scales, w, b, gain, out_0, 
             nc.sync.dma_start(out=raw[:], in_=rows.rearrange("(p j) c -> p j c", j=PACK))
             w_raw[k, g] = raw
 
-        def load_x(c, ks):
-            codes = keep.tile([P, len(ks), CHUNK], U32, name="x_%d_%d" % (c, ks[0]), align_bytes=64)
+        def load_x(c, part):
+            lo, hi = part
+            codes = keep.tile([P, PASSES, hi - lo], U32, name="x_%d_%d" % (c, lo), align_bytes=64)
             src = x_words.rearrange("k p n t -> p k (n t)")
-            src = src[:, ks[0]:ks[-1] + 1, c * CHUNK * PACK:(c + 1) * CHUNK * PACK]
+            src = src[:, :, (c * CHUNK + lo) * PACK:(c * CHUNK + hi) * PACK]
             nc.sync.dma_start(out=codes[:].bitcast(I32), in_=src.bitcast(I32))
-            for i, k in enumerate(ks):
-                x_codes[c, k] = codes[:, i, :]
+            x_codes[c, lo] = codes
+
+        def x_operand(c, k, part):
+            lo, hi = part
+            if (c, lo) in x_codes:
+                return x_codes[c, lo][:, k, 0:hi - lo]
+            return x_codes[c, 0][:, k, lo:hi]
 
         def load_x_scales(plane, n0, n1):
             for q in range(4):
@@ -72,24 +80,25 @@ def tile_scaled_tanh_pooler_g6_kernel(tc, x_words, x_scales, w, b, gain, out_0, 
                     in_=x_scales[:, 4 * q:4 * q + 4, n0:n1].bitcast(I32),
                 )
 
-        def x_plane(c, k):
-            if c == 0:
-                return xs_first[4 * k:P, :]
-            return xs_rest[4 * k:P, (c - 1) * CHUNK:c * CHUNK]
+        def x_plane(c, k, part):
+            lo, hi = part
+            plane = xs_first if c < CHUNKS // 2 else xs_rest
+            n0 = (c % (CHUNKS // 2)) * CHUNK
+            return plane[4 * k:P, n0 + lo:n0 + hi]
 
         load_w(0, 0)
-        load_x(0, [0])
-        load_x_scales(xs_first, 0, CHUNK)
         load_w(1, 0)
+        load_x_scales(xs_first, 0, M // 2)
+        load_x(0, HALVES[0])
         nc.sync.dma_start(out=bias[:], in_=b.rearrange("(g p t) -> p g t", p=P, t=PACK))
-        load_x(0, [1])
+        load_x(0, HALVES[1])
         nc.sync.dma_start(out=gains[:], in_=gain.rearrange("(g p t) -> p g t", p=P, t=PACK))
-        load_x(1, [0, 1])
-        load_x_scales(xs_rest, CHUNK, M)
+        load_x(1, WHOLE)
         load_w(0, 1)
+        load_x_scales(xs_rest, M // 2, M)
+        load_x(2, WHOLE)
         load_w(1, 1)
-        load_x(2, [0, 1])
-        load_x(3, [0, 1])
+        load_x(3, WHOLE)
 
         w_grouped = {}
         w_codes = {}
@@ -118,74 +127,89 @@ def tile_scaled_tanh_pooler_g6_kernel(tc, x_words, x_scales, w, b, gain, out_0, 
                 w_scales[k, g, 2 * h + u] = scales[:, u * P:(u + 1) * P]
 
         acc = {}
-        y_t = [keep.tile([P, PACK, CHUNK], F32, name="y_t_%d" % s) for s in range(STEPS)]
+        y_t = {}
+        for s in range(STEPS):
+            for lo, hi in (HALVES if s in (0, STEPS - 1) else (WHOLE,)):
+                y_t[s, lo] = keep.tile([P, PACK, hi - lo], F32, name="y_t_%d_%d" % (s, lo))
         y_packed = {}
         y_codes = {}
         turned = {}
         y_scales = [keep.tile([P, M], U8, name="y_scales_%d" % g, align_bytes=64) for g in range(GROUPS)]
 
-        def mx_pass(s, t, k):
+        def multiply(s, slots, part=WHOLE):
             g, c = divmod(s, CHUNKS)
-            if k == 0:
-                acc[s, t] = psum.tile([P, CHUNK], F32, name="acc_%d" % t)
-            nc.tensor.matmul_mx(
-                out=acc[s, t][:],
-                lhsT=w_codes[k, g, t].bitcast(FP8X4),
-                lhsT_scale=w_scales[k, g, t],
-                rhs=x_codes[c, k].bitcast(FP8X4),
-                rhs_scale=x_plane(c, k),
-                start=(k == 0),
-                stop=(k == PASSES - 1),
-            )
-
-        def multiply(s, slots):
             for t in slots:
-                for k in range(PASSES):
-                    mx_pass(s, t, k)
+                acc[s, t] = psum.tile([P, part[1] - part[0]], F32, name="acc_%d" % t)
+                for piece in (HALVES if c == 0 and part == WHOLE else (part,)):
+                    for k in range(PASSES):
+                        nc.tensor.matmul_mx(
+                            out=acc[s, t][:, piece[0] - part[0]:piece[1] - part[0]],
+                            lhsT=w_codes[k, g, t].bitcast(FP8X4),
+                            lhsT_scale=w_scales[k, g, t],
+                            rhs=x_operand(c, k, piece).bitcast(FP8X4),
+                            rhs_scale=x_plane(c, k, piece),
+                            start=(k == 0),
+                            stop=(k == PASSES - 1),
+                        )
 
-        def tanh(s, t):
+        def tanh(s, slots, part=WHOLE):
             g = s // CHUNKS
-            nc.scalar.activation(out=y_t[s][:, t, :], in_=acc[s, t][:], func=ACT.Tanh, bias=bias[:, g, t:t + 1])
+            for t in slots:
+                nc.scalar.activation(
+                    out=y_t[s, part[0]][:, t, :], in_=acc[s, t][:], func=ACT.Tanh, bias=bias[:, g, t:t + 1]
+                )
 
-        def scale(s, t):
+        def scale(s, slots, part=WHOLE):
             g = s // CHUNKS
-            nc.vector.tensor_scalar(
-                out=y_t[s][:, t, :], in0=y_t[s][:, t, :], scalar1=gains[:, g, t:t + 1], scalar2=None, op0=ALU.mult
-            )
+            for t in slots:
+                nc.vector.tensor_scalar(
+                    out=y_t[s, part[0]][:, t, :],
+                    in0=y_t[s, part[0]][:, t, :],
+                    scalar1=gains[:, g, t:t + 1],
+                    scalar2=None,
+                    op0=ALU.mult,
+                )
 
-        def interleave_y(s):
-            y_packed[s] = work.tile([P, CHUNK, PACK], BF16, name="y_packed", align_bytes=64)
+        def interleave_y(s, part=WHOLE):
+            lo, hi = part
+            packed = work.tile([P, hi - lo, PACK], BF16, name="y_packed", align_bytes=64)
             nc.vector.tensor_copy(
-                out=y_packed[s][:].rearrange("p (c i) t -> p c t i", i=2),
-                in_=y_t[s][:].rearrange("p t (c i) -> p c t i", i=2),
+                out=packed[:].rearrange("p (c i) t -> p c t i", i=2),
+                in_=y_t[s, lo][:].rearrange("p t (c i) -> p c t i", i=2),
             )
+            y_packed[s, lo] = packed
 
-        def quantize_y(s):
+        def quantize_y(s, part=WHOLE):
             g, c = divmod(s, CHUNKS)
-            codes = keep.tile([P, CHUNK], U32, name="y_codes_%d" % s, align_bytes=64)
+            lo, hi = part
+            codes = keep.tile([P, hi - lo], U32, name="y_codes_%d_%d" % (s, lo), align_bytes=64)
             nc.vector.quantize_mx(
                 out=codes[:].bitcast(FP8X4),
-                scales=y_scales[g][:, c * CHUNK:(c + 1) * CHUNK],
-                in_=y_packed[s][:].rearrange("p n t -> p (n t)"),
+                scales=y_scales[g][:, c * CHUNK + lo:c * CHUNK + hi],
+                in_=y_packed[s, lo][:].rearrange("p n t -> p (n t)"),
             )
-            y_codes[s] = codes
+            y_codes[s, lo] = codes
 
-        def store_planes(s):
+        def store_planes(s, part=WHOLE):
             g, c = divmod(s, CHUNKS)
-            dst = out_1[g].rearrange("p n t -> p (n t)")[:, c * CHUNK * PACK:(c + 1) * CHUNK * PACK]
-            nc.sync.dma_start(out=dst.bitcast(I32), in_=y_codes[s][:].bitcast(I32))
-            if c == CHUNKS - 1:
-                for q in range(4):
-                    nc.sync.dma_start(
-                        out=out_2[g, 4 * q:4 * q + 4, :].bitcast(I32),
-                        in_=y_scales[g][32 * q:32 * q + 4, :].bitcast(I32),
-                    )
+            lo, hi = part
+            dst = out_1[g].rearrange("p n t -> p (n t)")[:, (c * CHUNK + lo) * PACK:(c * CHUNK + hi) * PACK]
+            nc.sync.dma_start(out=dst.bitcast(I32), in_=y_codes[s, lo][:].bitcast(I32))
+
+        def store_scales(g):
+            for q in range(4):
+                nc.sync.dma_start(
+                    out=out_2[g, 4 * q:4 * q + 4, :].bitcast(I32),
+                    in_=y_scales[g][32 * q:32 * q + 4, :].bitcast(I32),
+                )
 
         def transpose(s, blocks):
-            for j in blocks:
-                turned[s, j] = psum.tile([P, PACK, P], F32, name="turned_%d" % j)
+            for j, bank in blocks:
+                turned[s, j] = psum.tile([P, PACK, P], F32, name="turned_%d" % bank)
+                lo = CHUNK // 2 if (s, CHUNK // 2) in y_t and j * P >= CHUNK // 2 else 0
                 for t in range(PACK):
-                    nc.tensor.transpose(turned[s, j][:, t, :], y_t[s][:, t, j * P:(j + 1) * P], ident[:])
+                    src = y_t[s, lo][:, t, j * P - lo:(j + 1) * P - lo]
+                    nc.tensor.transpose(turned[s, j][:, t, :], src, ident[:])
 
         def emit(s, j, on_scalar):
             g, c = divmod(s, CHUNKS)
@@ -202,60 +226,101 @@ def tile_scaled_tanh_pooler_g6_kernel(tc, x_words, x_scales, w, b, gain, out_0, 
 
         def last_first(order):
             return order[-1:] + order[:-1]
-
-        for k in range(PASSES):
-            interleave_w(k, 0, 0, on_scalar=False)
-            interleave_w(k, 0, 1, on_scalar=True)
-            for h in range(2):
-                quantize_w(k, 0, h)
-            for t in range(PACK):
-                mx_pass(0, t, k)
-
-        later = [(k, 1, h) for k in range(PASSES) for h in range(2)]
-
+        def swap_pairs(order):
+            return [order[1], order[0], order[3], order[2]]
+        NV = [0,0,1,1,1,1,1]
+        interleave_w(0, 0, 0, on_scalar=False)
+        interleave_w(0, 0, 1, on_scalar=True)
+        quantize_w(0, 0, 0)
+        interleave_w(1, 0, 0, on_scalar=False)
+        interleave_w(1, 0, 1, on_scalar=True)
+        quantize_w(0, 0, 1)
+        quantize_w(1, 0, 0)
+        quantize_w(1, 0, 1)
         slots = list(range(PACK))
-        for t in slots:
-            tanh(0, t)
-            if t == slots[-1]:
-                interleave_w(*later[0], on_scalar=False)
-            scale(0, t)
-        quantize_w(*later[0])
+        first, second = HALVES
+        multiply(0, slots, first)
+        tanh(0, slots, first)
+        scale(0, slots, first)
+        multiply(0, slots, second)
+        interleave_y(0, first)
+        tanh(0, slots, second)
+        scale(0, slots, second)
         multiply(1, slots)
-
-        blocks = list(range(BLOCKS))
-        for s in range(STEPS - 1):
-            piece = later[s + 1] if s + 1 < len(later) else None
-            transpose(s, blocks)
-            if piece:
-                interleave_w(*piece, on_scalar=False)
+        quantize_y(0, first)
+        banks = list(range(BLOCKS))
+        for s in range(STEPS - 2):
+            transpose(s, [(j, j) for j in banks])
+            on_vector = banks[:NV[s]]
+            if s == 0:
+                interleave_y(0, second)
+                interleave_w(0, 1, 0, on_scalar=False)
+                quantize_y(0, second)
+            elif s == 1:
+                interleave_w(0, 1, 1, on_scalar=False)
                 interleave_y(s)
-                quantize_w(*piece)
-                on_vector = []
+                quantize_w(0, 1, 1)
+                interleave_w(1, 1, 0, on_scalar=False)
+            elif s == 2:
+                interleave_w(1, 1, 1, on_scalar=False)
+                interleave_y(s)
+                quantize_w(1, 1, 1)
             else:
                 interleave_y(s)
-                on_vector = blocks[:1]
-                emit(s, blocks[0], on_scalar=False)
+            for j in on_vector:
+                emit(s, j, on_scalar=False)
             if s > 0:
-                slots = last_first(slots)
-            for t in slots:
-                tanh(s + 1, t)
-            for t in (last_first(slots) if s + 2 < STEPS else slots):
-                scale(s + 1, t)
-            quantize_y(s)
-            if s + 2 < STEPS:
+                slots = swap_pairs(slots)
+            tanh(s + 1, slots)
+            scale(s + 1, last_first(slots) if s + 3 < STEPS else slots)
+            if s == 0:
+                quantize_w(0, 1, 0)
+            else:
+                if s == 1:
+                    quantize_w(1, 1, 0)
+                quantize_y(s)
+            if s + 3 < STEPS:
                 multiply(s + 2, slots)
-            on_scalar = last_first(blocks[len(on_vector):])
+            else:
+                multiply(s + 2, slots[:2], first)
+            on_scalar = banks[len(on_vector):]
+            if s > 0:
+                on_scalar = last_first(on_scalar)
             for j in on_scalar:
                 emit(s, j, on_scalar=True)
-            store_planes(s)
-            blocks = on_vector + on_scalar
-
-        s = STEPS - 1
-        transpose(s, blocks)
+            if s == 0:
+                store_planes(0, first)
+                store_planes(0, second)
+            else:
+                store_planes(s)
+            if s == CHUNKS - 1:
+                store_scales(0)
+            banks = on_vector + on_scalar
+        s, last = STEPS - 2, STEPS - 1
+        transpose(s, [(j, j) for j in banks[:4]])
+        multiply(last, slots[2:], first)
         interleave_y(s)
-        emit(s, blocks[0], on_scalar=True)
-        emit(s, blocks[1], on_scalar=True)
-        emit(s, blocks[2], on_scalar=True)
+        for j in banks[:BLOCKS - NV[s]]:
+            emit(s, j, on_scalar=True)
+        for j in banks[BLOCKS - NV[s]:]:
+            emit(s, j, on_scalar=False)
         quantize_y(s)
-        emit(s, blocks[3], on_scalar=True)
         store_planes(s)
+        tanh(last, slots, first)
+        scale(last, slots, first)
+        multiply(last, slots, second)
+        transpose(last, [(0, banks[0]), (1, banks[1])])
+        interleave_y(last, first)
+        tanh(last, slots, second)
+        scale(last, slots, second)
+        transpose(last, [(2, banks[2]), (3, banks[3])])
+        quantize_y(last, first)
+        emit(last, 0, on_scalar=True)
+        store_planes(last, first)
+        emit(last, 1, on_scalar=True)
+        interleave_y(last, second)
+        emit(last, 2, on_scalar=True)
+        quantize_y(last, second)
+        store_planes(last, second)
+        emit(last, 3, on_scalar=True)
+        store_scales(1)

@@ -17,15 +17,29 @@ ALU = mybir.AluOpType
 
 P = 128
 PACK = 4
-GROUP = P * PACK
-PASSES = K // GROUP
-GROUPS = N // GROUP
+SPAN = P * PACK
+PASSES = K // SPAN
+GROUPS = N // SPAN
+QUADRANTS = 4
 CHUNK = 512
 CHUNKS = M // CHUNK
 STEPS = GROUPS * CHUNKS
+LAST = STEPS - 1
 BLOCKS = CHUNK // P
 WHOLE = (0, CHUNK)
-HALVES = ((0, CHUNK // 2), (CHUNK // 2, CHUNK))
+FIRST_HALF = (0, CHUNK // 2)
+SECOND_HALF = (CHUNK // 2, CHUNK)
+HALVES = (FIRST_HALF, SECOND_HALF)
+VECTOR_COPIES_FROM = 2
+EARLY_SLOTS = 3
+
+
+def last_first(order):
+    return order[-1:] + order[:-1]
+
+
+def swap_pairs(order):
+    return [order[1], order[0], order[3], order[2]]
 
 
 def tile_scaled_tanh_pooler_g6_kernel(tc, x_words, x_scales, w, b, gain, out_0, out_1, out_2):
@@ -43,19 +57,15 @@ def tile_scaled_tanh_pooler_g6_kernel(tc, x_words, x_scales, w, b, gain, out_0, 
 
         xs_first = keep.tile([P, M // 2], U8, name="xs_first", align_bytes=64)
         xs_rest = keep.tile([P, M // 2], U8, name="xs_rest", align_bytes=64)
-        warm = keep.tile([P, 8], F32, name="warm")
-        warm_out = keep.tile([P, 8], F32, name="warm_out")
         nc.vector.memset(xs_first[:].bitcast(I32), 0)
-        nc.vector.memset(warm[:], 0.0)
         nc.vector.memset(xs_rest[:].bitcast(I32), 0)
-        nc.scalar.activation(out=warm_out[:], in_=warm[:], func=ACT.Tanh)
 
         w_raw = {}
         x_codes = {}
 
         def load_w(k, g):
-            raw = keep.tile([P, PACK, GROUP], BF16, name="w_raw_%d_%d" % (k, g))
-            rows = w[k * GROUP:(k + 1) * GROUP, g * GROUP:(g + 1) * GROUP]
+            raw = keep.tile([P, PACK, SPAN], BF16, name="w_raw_%d_%d" % (k, g))
+            rows = w[k * SPAN:(k + 1) * SPAN, g * SPAN:(g + 1) * SPAN]
             nc.sync.dma_start(out=raw[:], in_=rows.rearrange("(p j) c -> p j c", j=PACK))
             w_raw[k, g] = raw
 
@@ -65,33 +75,27 @@ def tile_scaled_tanh_pooler_g6_kernel(tc, x_words, x_scales, w, b, gain, out_0, 
             src = x_words.rearrange("k p n t -> p k (n t)")
             src = src[:, :, (c * CHUNK + lo) * PACK:(c * CHUNK + hi) * PACK]
             nc.sync.dma_start(out=codes[:].bitcast(I32), in_=src.bitcast(I32))
-            x_codes[c, lo] = codes
+            x_codes[c, part] = codes
 
-        def x_operand(c, k, part):
-            lo, hi = part
-            if (c, lo) in x_codes:
-                return x_codes[c, lo][:, k, 0:hi - lo]
-            return x_codes[c, 0][:, k, lo:hi]
-
-        def load_x_scales(plane, n0, n1):
-            for q in range(4):
+        def load_x_scales(tile, n0, n1):
+            for q in range(QUADRANTS):
                 nc.sync.dma_start(
-                    out=plane[32 * q:32 * q + 4 * PASSES, :].bitcast(I32),
+                    out=tile[32 * q:32 * q + 4 * PASSES, :].bitcast(I32),
                     in_=x_scales[:, 4 * q:4 * q + 4, n0:n1].bitcast(I32),
                 )
 
-        def x_plane(c, k, part):
+        def x_scale_operand(c, k, part):
             lo, hi = part
-            plane = xs_first if c < CHUNKS // 2 else xs_rest
+            tile = xs_first if c < CHUNKS // 2 else xs_rest
             n0 = (c % (CHUNKS // 2)) * CHUNK
-            return plane[4 * k:P, n0 + lo:n0 + hi]
+            return tile[4 * k:P, n0 + lo:n0 + hi]
 
         load_w(0, 0)
         load_w(1, 0)
         load_x_scales(xs_first, 0, M // 2)
-        load_x(0, HALVES[0])
+        load_x(0, FIRST_HALF)
         nc.sync.dma_start(out=bias[:], in_=b.rearrange("(g p t) -> p g t", p=P, t=PACK))
-        load_x(0, HALVES[1])
+        load_x(0, SECOND_HALF)
         nc.sync.dma_start(out=gains[:], in_=gain.rearrange("(g p t) -> p g t", p=P, t=PACK))
         load_x(1, WHOLE)
         load_w(0, 1)
@@ -104,32 +108,44 @@ def tile_scaled_tanh_pooler_g6_kernel(tc, x_words, x_scales, w, b, gain, out_0, 
         w_codes = {}
         w_scales = {}
 
-        def interleave_w(k, g, h, on_scalar):
+        def interleave_w_pair(k, g, h, on_scalar):
             grouped = keep.tile([P, 2, P, PACK], BF16, name="w_grouped_%d_%d_%d" % (k, g, h), align_bytes=64)
-            src = w_raw[k, g][:].rearrange("p j (a m h u) -> p h a j m u", m=2, h=2, u=2)[:, h]
-            dst = grouped[:].rearrange("p u (a m) j -> p a j m u", m=2)
             if on_scalar:
-                nc.scalar.copy(out=dst, in_=src)
+                src = w_raw[k, g][:].rearrange("p j (m h u) -> p h m j u", h=2, u=2)[:, h]
+                dst = grouped[:].rearrange("p u m j -> p m j u")
+                nc.scalar.activation(out=dst, in_=src, func=ACT.Copy)
             else:
+                src = w_raw[k, g][:].rearrange("p j (a m h u) -> p h a j m u", m=2, h=2, u=2)[:, h]
+                dst = grouped[:].rearrange("p u (a m) j -> p a j m u", m=2)
                 nc.vector.tensor_copy(out=dst, in_=src)
-            w_grouped[k, g, h] = grouped
+            w_grouped[k, g, 2 * h] = grouped
 
-        def quantize_w(k, g, h):
-            codes = keep.tile([P, 2 * P], U32, name="w_codes_%d_%d_%d" % (k, g, h), align_bytes=64)
-            scales = keep.tile([P, 2 * P], U8, name="w_scales_%d_%d_%d" % (k, g, h), align_bytes=64)
+        def interleave_w(k, g):
+            grouped = keep.tile([P, PACK, P, PACK], BF16, name="w_grouped_%d_%d" % (k, g), align_bytes=64)
+            nc.vector.tensor_copy(
+                out=grouped[:].rearrange("p (h u) m j -> p h m j u", u=2),
+                in_=w_raw[k, g][:].rearrange("p j (m h u) -> p h m j u", h=2, u=2),
+            )
+            w_grouped[k, g, 0] = grouped
+
+        def quantize_w(k, g, t0):
+            grouped = w_grouped[k, g, t0]
+            count = grouped.shape[1]
+            codes = keep.tile([P, count * P], U32, name="w_codes_%d_%d_%d" % (k, g, t0), align_bytes=64)
+            scales = keep.tile([P, count * P], U8, name="w_scales_%d_%d_%d" % (k, g, t0), align_bytes=64)
             nc.vector.quantize_mx(
                 out=codes[:].bitcast(FP8X4),
                 scales=scales[:],
-                in_=w_grouped[k, g, h][:].rearrange("p u m j -> p (u m j)"),
+                in_=grouped[:].rearrange("p u m j -> p (u m j)"),
             )
-            for u in range(2):
-                w_codes[k, g, 2 * h + u] = codes[:, u * P:(u + 1) * P]
-                w_scales[k, g, 2 * h + u] = scales[:, u * P:(u + 1) * P]
+            for u in range(count):
+                w_codes[k, g, t0 + u] = codes[:, u * P:(u + 1) * P]
+                w_scales[k, g, t0 + u] = scales[:, u * P:(u + 1) * P]
 
         acc = {}
         y_t = {}
         for s in range(STEPS):
-            for lo, hi in (HALVES if s in (0, STEPS - 1) else (WHOLE,)):
+            for lo, hi in (HALVES if s in (0, LAST) else (WHOLE,)):
                 y_t[s, lo] = keep.tile([P, PACK, hi - lo], F32, name="y_t_%d_%d" % (s, lo))
         y_packed = {}
         y_codes = {}
@@ -146,8 +162,8 @@ def tile_scaled_tanh_pooler_g6_kernel(tc, x_words, x_scales, w, b, gain, out_0, 
                             out=acc[s, t][:, piece[0] - part[0]:piece[1] - part[0]],
                             lhsT=w_codes[k, g, t].bitcast(FP8X4),
                             lhsT_scale=w_scales[k, g, t],
-                            rhs=x_operand(c, k, piece).bitcast(FP8X4),
-                            rhs_scale=x_plane(c, k, piece),
+                            rhs=x_codes[c, piece][:, k, :].bitcast(FP8X4),
+                            rhs_scale=x_scale_operand(c, k, piece),
                             start=(k == 0),
                             stop=(k == PASSES - 1),
                         )
@@ -155,8 +171,9 @@ def tile_scaled_tanh_pooler_g6_kernel(tc, x_words, x_scales, w, b, gain, out_0, 
         def tanh(s, slots, part=WHOLE):
             g = s // CHUNKS
             for t in slots:
+                sums = acc[s, t][:, part[0]:part[1]] if s == LAST else acc[s, t][:]
                 nc.scalar.activation(
-                    out=y_t[s, part[0]][:, t, :], in_=acc[s, t][:], func=ACT.Tanh, bias=bias[:, g, t:t + 1]
+                    out=y_t[s, part[0]][:, t, :], in_=sums, func=ACT.Tanh, bias=bias[:, g, t:t + 1]
                 )
 
         def scale(s, slots, part=WHOLE):
@@ -190,26 +207,25 @@ def tile_scaled_tanh_pooler_g6_kernel(tc, x_words, x_scales, w, b, gain, out_0, 
             )
             y_codes[s, lo] = codes
 
-        def store_planes(s, part=WHOLE):
+        def store_codes(s, part=WHOLE):
             g, c = divmod(s, CHUNKS)
             lo, hi = part
             dst = out_1[g].rearrange("p n t -> p (n t)")[:, (c * CHUNK + lo) * PACK:(c * CHUNK + hi) * PACK]
             nc.sync.dma_start(out=dst.bitcast(I32), in_=y_codes[s, lo][:].bitcast(I32))
 
         def store_scales(g):
-            for q in range(4):
+            for q in range(QUADRANTS):
                 nc.sync.dma_start(
                     out=out_2[g, 4 * q:4 * q + 4, :].bitcast(I32),
                     in_=y_scales[g][32 * q:32 * q + 4, :].bitcast(I32),
                 )
 
-        def transpose(s, blocks):
-            for j, bank in blocks:
-                turned[s, j] = psum.tile([P, PACK, P], F32, name="turned_%d" % bank)
-                lo = CHUNK // 2 if (s, CHUNK // 2) in y_t and j * P >= CHUNK // 2 else 0
-                for t in range(PACK):
-                    src = y_t[s, lo][:, t, j * P - lo:(j + 1) * P - lo]
-                    nc.tensor.transpose(turned[s, j][:, t, :], src, ident[:])
+        def transpose(s, j, bank):
+            turned[s, j] = psum.tile([P, PACK, P], F32, name="turned_%d" % bank)
+            lo = CHUNK // 2 if s in (0, LAST) and j * P >= CHUNK // 2 else 0
+            for t in range(PACK):
+                src = y_t[s, lo][:, t, j * P - lo:(j + 1) * P - lo]
+                nc.tensor.transpose(turned[s, j][:, t, :], src, ident[:])
 
         def emit(s, j, on_scalar):
             g, c = divmod(s, CHUNKS)
@@ -221,106 +237,92 @@ def tile_scaled_tanh_pooler_g6_kernel(tc, x_words, x_scales, w, b, gain, out_0, 
                 nc.vector.tensor_copy(out=rows[:], in_=src)
             n0 = c * CHUNK + j * P
             nc.sync.dma_start(
-                out=out_0[n0:n0 + P, g * GROUP:(g + 1) * GROUP], in_=rows[:].rearrange("n m t -> n (m t)")
+                out=out_0[n0:n0 + P, g * SPAN:(g + 1) * SPAN], in_=rows[:].rearrange("n m t -> n (m t)")
             )
 
-        def last_first(order):
-            return order[-1:] + order[:-1]
-        def swap_pairs(order):
-            return [order[1], order[0], order[3], order[2]]
-        NV = [0,0,1,1,1,1,1]
-        interleave_w(0, 0, 0, on_scalar=False)
-        interleave_w(0, 0, 1, on_scalar=True)
+        interleave_w_pair(0, 0, 0, on_scalar=False)
+        interleave_w_pair(0, 0, 1, on_scalar=True)
         quantize_w(0, 0, 0)
-        interleave_w(1, 0, 0, on_scalar=False)
-        interleave_w(1, 0, 1, on_scalar=True)
-        quantize_w(0, 0, 1)
+        interleave_w_pair(1, 0, 0, on_scalar=False)
+        interleave_w_pair(1, 0, 1, on_scalar=True)
+        quantize_w(0, 0, 2)
         quantize_w(1, 0, 0)
-        quantize_w(1, 0, 1)
+        quantize_w(1, 0, 2)
+
         slots = list(range(PACK))
-        first, second = HALVES
-        multiply(0, slots, first)
-        tanh(0, slots, first)
-        scale(0, slots, first)
-        multiply(0, slots, second)
-        interleave_y(0, first)
-        tanh(0, slots, second)
-        scale(0, slots, second)
+        multiply(0, slots, FIRST_HALF)
+        tanh(0, slots, FIRST_HALF)
+        scale(0, slots, FIRST_HALF)
+        multiply(0, slots, SECOND_HALF)
+        interleave_y(0, FIRST_HALF)
+        tanh(0, slots, SECOND_HALF)
+        scale(0, slots, SECOND_HALF)
         multiply(1, slots)
-        quantize_y(0, first)
+        quantize_y(0, FIRST_HALF)
+
         banks = list(range(BLOCKS))
         for s in range(STEPS - 2):
-            transpose(s, [(j, j) for j in banks])
-            on_vector = banks[:NV[s]]
+            for j in banks:
+                transpose(s, j, j)
             if s == 0:
-                interleave_y(0, second)
-                interleave_w(0, 1, 0, on_scalar=False)
-                quantize_y(0, second)
+                interleave_y(0, SECOND_HALF)
+                interleave_w(0, 1)
+                quantize_y(0, SECOND_HALF)
             elif s == 1:
-                interleave_w(0, 1, 1, on_scalar=False)
+                interleave_w(1, 1)
                 interleave_y(s)
-                quantize_w(0, 1, 1)
-                interleave_w(1, 1, 0, on_scalar=False)
-            elif s == 2:
-                interleave_w(1, 1, 1, on_scalar=False)
-                interleave_y(s)
-                quantize_w(1, 1, 1)
             else:
                 interleave_y(s)
+            on_vector = banks[:1] if s >= VECTOR_COPIES_FROM else []
             for j in on_vector:
                 emit(s, j, on_scalar=False)
             if s > 0:
                 slots = swap_pairs(slots)
             tanh(s + 1, slots)
-            scale(s + 1, last_first(slots) if s + 3 < STEPS else slots)
-            if s == 0:
-                quantize_w(0, 1, 0)
-            else:
-                if s == 1:
-                    quantize_w(1, 1, 0)
+            scale(s + 1, last_first(slots) if s + 2 < LAST else slots)
+            if s < PASSES:
+                quantize_w(s, 1, 0)
+            if s > 0:
                 quantize_y(s)
-            if s + 3 < STEPS:
-                multiply(s + 2, slots)
-            else:
-                multiply(s + 2, slots[:2], first)
+            multiply(s + 2, slots if s + 2 < LAST else slots[:EARLY_SLOTS])
             on_scalar = banks[len(on_vector):]
             if s > 0:
                 on_scalar = last_first(on_scalar)
             for j in on_scalar:
                 emit(s, j, on_scalar=True)
-            if s == 0:
-                store_planes(0, first)
-                store_planes(0, second)
-            else:
-                store_planes(s)
+            for part in (HALVES if s == 0 else (WHOLE,)):
+                store_codes(s, part)
             if s == CHUNKS - 1:
                 store_scales(0)
             banks = on_vector + on_scalar
-        s, last = STEPS - 2, STEPS - 1
-        transpose(s, [(j, j) for j in banks[:4]])
-        multiply(last, slots[2:], first)
+
+        s = LAST - 1
+        for j in banks:
+            transpose(s, j, j)
+        multiply(LAST, slots[EARLY_SLOTS:])
         interleave_y(s)
-        for j in banks[:BLOCKS - NV[s]]:
+        for j in banks[:-1]:
             emit(s, j, on_scalar=True)
-        for j in banks[BLOCKS - NV[s]:]:
-            emit(s, j, on_scalar=False)
+        emit(s, banks[-1], on_scalar=False)
         quantize_y(s)
-        store_planes(s)
-        tanh(last, slots, first)
-        scale(last, slots, first)
-        multiply(last, slots, second)
-        transpose(last, [(0, banks[0]), (1, banks[1])])
-        interleave_y(last, first)
-        tanh(last, slots, second)
-        scale(last, slots, second)
-        transpose(last, [(2, banks[2]), (3, banks[3])])
-        quantize_y(last, first)
-        emit(last, 0, on_scalar=True)
-        store_planes(last, first)
-        emit(last, 1, on_scalar=True)
-        interleave_y(last, second)
-        emit(last, 2, on_scalar=True)
-        quantize_y(last, second)
-        store_planes(last, second)
-        emit(last, 3, on_scalar=True)
-        store_scales(1)
+        store_codes(s)
+
+        tanh(LAST, slots, FIRST_HALF)
+        scale(LAST, slots, FIRST_HALF)
+        for j in range(BLOCKS // 2):
+            transpose(LAST, j, banks[j])
+        interleave_y(LAST, FIRST_HALF)
+        tanh(LAST, slots, SECOND_HALF)
+        scale(LAST, slots, SECOND_HALF)
+        for j in range(BLOCKS // 2, BLOCKS):
+            transpose(LAST, j, banks[j])
+        quantize_y(LAST, FIRST_HALF)
+        emit(LAST, 0, on_scalar=True)
+        store_codes(LAST, FIRST_HALF)
+        emit(LAST, 1, on_scalar=True)
+        interleave_y(LAST, SECOND_HALF)
+        emit(LAST, 2, on_scalar=True)
+        quantize_y(LAST, SECOND_HALF)
+        store_codes(LAST, SECOND_HALF)
+        store_scales(GROUPS - 1)
+        emit(LAST, 3, on_scalar=True)

from contextlib import ExitStack

import concourse.mybir as mybir
from concourse.masks import make_identity

M, K, N = 2048, 1024, 1024
FLOPS = 2 * M * K * N

F32 = mybir.dt.float32
BF16 = mybir.dt.bfloat16
I32 = mybir.dt.int32
U32 = mybir.dt.uint32
U8 = mybir.dt.uint8
FP8X4 = mybir.dt.float8_e4m3fn_x4
ACT = mybir.ActivationFunctionType
ALU = mybir.AluOpType

P = 128
PACK = 4
SPAN = P * PACK
PASSES = K // SPAN
GROUPS = N // SPAN
QUADRANTS = 4
CHUNK = 512
CHUNKS = M // CHUNK
STEPS = GROUPS * CHUNKS
LAST = STEPS - 1
BLOCKS = CHUNK // P
WHOLE = (0, CHUNK)
FIRST_HALF = (0, CHUNK // 2)
SECOND_HALF = (CHUNK // 2, CHUNK)
HALVES = (FIRST_HALF, SECOND_HALF)
VECTOR_COPIES_FROM = 2
EARLY_SLOTS = 3


def last_first(order):
    return order[-1:] + order[:-1]


def swap_pairs(order):
    return [order[1], order[0], order[3], order[2]]


def tile_scaled_tanh_pooler_g6_kernel(tc, x_words, x_scales, w, b, gain, out_0, out_1, out_2):
    nc = tc.nc
    with ExitStack() as ctx:
        keep = ctx.enter_context(tc.tile_pool(name="keep", bufs=1))
        work = ctx.enter_context(tc.tile_pool(name="work", bufs=2))
        psum = ctx.enter_context(tc.psum_pool(name="psum", bufs=1))
        ctx.enter_context(tc.manual_schedule())

        bias = keep.tile([P, GROUPS, PACK], BF16, name="bias")
        gains = keep.tile([P, GROUPS, PACK], BF16, name="gains")
        ident = keep.tile([P, P], F32, name="ident")
        make_identity(nc, ident[:])

        xs_first = keep.tile([P, M // 2], U8, name="xs_first", align_bytes=64)
        xs_rest = keep.tile([P, M // 2], U8, name="xs_rest", align_bytes=64)
        nc.vector.memset(xs_first[:].bitcast(I32), 0)
        nc.vector.memset(xs_rest[:].bitcast(I32), 0)

        w_raw = {}
        x_codes = {}

        def load_w(k, g):
            raw = keep.tile([P, PACK, SPAN], BF16, name="w_raw_%d_%d" % (k, g))
            rows = w[k * SPAN:(k + 1) * SPAN, g * SPAN:(g + 1) * SPAN]
            nc.sync.dma_start(out=raw[:], in_=rows.rearrange("(p j) c -> p j c", j=PACK))
            w_raw[k, g] = raw

        def load_x(c, part):
            lo, hi = part
            codes = keep.tile([P, PASSES, hi - lo], U32, name="x_%d_%d" % (c, lo), align_bytes=64)
            src = x_words.rearrange("k p n t -> p k (n t)")
            src = src[:, :, (c * CHUNK + lo) * PACK:(c * CHUNK + hi) * PACK]
            nc.sync.dma_start(out=codes[:].bitcast(I32), in_=src.bitcast(I32))
            x_codes[c, part] = codes

        def load_x_scales(tile, n0, n1):
            for q in range(QUADRANTS):
                nc.sync.dma_start(
                    out=tile[32 * q:32 * q + 4 * PASSES, :].bitcast(I32),
                    in_=x_scales[:, 4 * q:4 * q + 4, n0:n1].bitcast(I32),
                )

        def x_scale_operand(c, k, part):
            lo, hi = part
            tile = xs_first if c < CHUNKS // 2 else xs_rest
            n0 = (c % (CHUNKS // 2)) * CHUNK
            return tile[4 * k:P, n0 + lo:n0 + hi]

        load_w(0, 0)
        load_w(1, 0)
        load_x_scales(xs_first, 0, M // 2)
        load_x(0, FIRST_HALF)
        nc.sync.dma_start(out=bias[:], in_=b.rearrange("(g p t) -> p g t", p=P, t=PACK))
        load_x(0, SECOND_HALF)
        nc.sync.dma_start(out=gains[:], in_=gain.rearrange("(g p t) -> p g t", p=P, t=PACK))
        load_x(1, WHOLE)
        load_w(0, 1)
        load_x_scales(xs_rest, M // 2, M)
        load_x(2, WHOLE)
        load_w(1, 1)
        load_x(3, WHOLE)

        w_grouped = {}
        w_codes = {}
        w_scales = {}

        def interleave_w_pair(k, g, h, on_scalar):
            grouped = keep.tile([P, 2, P, PACK], BF16, name="w_grouped_%d_%d_%d" % (k, g, h), align_bytes=64)
            if on_scalar:
                src = w_raw[k, g][:].rearrange("p j (m h u) -> p h m j u", h=2, u=2)[:, h]
                dst = grouped[:].rearrange("p u m j -> p m j u")
                nc.scalar.activation(out=dst, in_=src, func=ACT.Copy)
            else:
                src = w_raw[k, g][:].rearrange("p j (a m h u) -> p h a j m u", m=2, h=2, u=2)[:, h]
                dst = grouped[:].rearrange("p u (a m) j -> p a j m u", m=2)
                nc.vector.tensor_copy(out=dst, in_=src)
            w_grouped[k, g, 2 * h] = grouped

        def interleave_w(k, g):
            grouped = keep.tile([P, PACK, P, PACK], BF16, name="w_grouped_%d_%d" % (k, g), align_bytes=64)
            nc.vector.tensor_copy(
                out=grouped[:].rearrange("p (h u) m j -> p h m j u", u=2),
                in_=w_raw[k, g][:].rearrange("p j (m h u) -> p h m j u", h=2, u=2),
            )
            w_grouped[k, g, 0] = grouped

        def quantize_w(k, g, t0):
            grouped = w_grouped[k, g, t0]
            count = grouped.shape[1]
            codes = keep.tile([P, count * P], U32, name="w_codes_%d_%d_%d" % (k, g, t0), align_bytes=64)
            scales = keep.tile([P, count * P], U8, name="w_scales_%d_%d_%d" % (k, g, t0), align_bytes=64)
            nc.vector.quantize_mx(
                out=codes[:].bitcast(FP8X4),
                scales=scales[:],
                in_=grouped[:].rearrange("p u m j -> p (u m j)"),
            )
            for u in range(count):
                w_codes[k, g, t0 + u] = codes[:, u * P:(u + 1) * P]
                w_scales[k, g, t0 + u] = scales[:, u * P:(u + 1) * P]

        acc = {}
        y_t = {}
        for s in range(STEPS):
            for lo, hi in (HALVES if s in (0, LAST) else (WHOLE,)):
                y_t[s, lo] = keep.tile([P, PACK, hi - lo], F32, name="y_t_%d_%d" % (s, lo))
        y_packed = {}
        y_codes = {}
        turned = {}
        y_scales = [keep.tile([P, M], U8, name="y_scales_%d" % g, align_bytes=64) for g in range(GROUPS)]

        def multiply(s, slots, part=WHOLE):
            g, c = divmod(s, CHUNKS)
            for t in slots:
                acc[s, t] = psum.tile([P, part[1] - part[0]], F32, name="acc_%d" % t)
                for piece in (HALVES if c == 0 and part == WHOLE else (part,)):
                    for k in range(PASSES):
                        nc.tensor.matmul_mx(
                            out=acc[s, t][:, piece[0] - part[0]:piece[1] - part[0]],
                            lhsT=w_codes[k, g, t].bitcast(FP8X4),
                            lhsT_scale=w_scales[k, g, t],
                            rhs=x_codes[c, piece][:, k, :].bitcast(FP8X4),
                            rhs_scale=x_scale_operand(c, k, piece),
                            start=(k == 0),
                            stop=(k == PASSES - 1),
                        )

        def tanh(s, slots, part=WHOLE):
            g = s // CHUNKS
            for t in slots:
                sums = acc[s, t][:, part[0]:part[1]] if s == LAST else acc[s, t][:]
                nc.scalar.activation(
                    out=y_t[s, part[0]][:, t, :], in_=sums, func=ACT.Tanh, bias=bias[:, g, t:t + 1]
                )

        def scale(s, slots, part=WHOLE):
            g = s // CHUNKS
            for t in slots:
                nc.vector.tensor_scalar(
                    out=y_t[s, part[0]][:, t, :],
                    in0=y_t[s, part[0]][:, t, :],
                    scalar1=gains[:, g, t:t + 1],
                    scalar2=None,
                    op0=ALU.mult,
                )

        def interleave_y(s, part=WHOLE):
            lo, hi = part
            packed = work.tile([P, hi - lo, PACK], BF16, name="y_packed", align_bytes=64)
            nc.vector.tensor_copy(
                out=packed[:].rearrange("p (c i) t -> p c t i", i=2),
                in_=y_t[s, lo][:].rearrange("p t (c i) -> p c t i", i=2),
            )
            y_packed[s, lo] = packed

        def quantize_y(s, part=WHOLE):
            g, c = divmod(s, CHUNKS)
            lo, hi = part
            codes = keep.tile([P, hi - lo], U32, name="y_codes_%d_%d" % (s, lo), align_bytes=64)
            nc.vector.quantize_mx(
                out=codes[:].bitcast(FP8X4),
                scales=y_scales[g][:, c * CHUNK + lo:c * CHUNK + hi],
                in_=y_packed[s, lo][:].rearrange("p n t -> p (n t)"),
            )
            y_codes[s, lo] = codes

        def store_codes(s, part=WHOLE):
            g, c = divmod(s, CHUNKS)
            lo, hi = part
            dst = out_1[g].rearrange("p n t -> p (n t)")[:, (c * CHUNK + lo) * PACK:(c * CHUNK + hi) * PACK]
            nc.sync.dma_start(out=dst.bitcast(I32), in_=y_codes[s, lo][:].bitcast(I32))

        def store_scales(g):
            for q in range(QUADRANTS):
                nc.sync.dma_start(
                    out=out_2[g, 4 * q:4 * q + 4, :].bitcast(I32),
                    in_=y_scales[g][32 * q:32 * q + 4, :].bitcast(I32),
                )

        def transpose(s, j, bank):
            turned[s, j] = psum.tile([P, PACK, P], F32, name="turned_%d" % bank)
            lo = CHUNK // 2 if s in (0, LAST) and j * P >= CHUNK // 2 else 0
            for t in range(PACK):
                src = y_t[s, lo][:, t, j * P - lo:(j + 1) * P - lo]
                nc.tensor.transpose(turned[s, j][:, t, :], src, ident[:])

        def emit(s, j, on_scalar):
            g, c = divmod(s, CHUNKS)
            rows = keep.tile([P, P, PACK], F32, name="rows_%d_%d" % (s, j))
            src = turned[s, j][:].rearrange("n t m -> n m t")
            if on_scalar:
                nc.scalar.copy(out=rows[:], in_=src)
            else:
                nc.vector.tensor_copy(out=rows[:], in_=src)
            n0 = c * CHUNK + j * P
            nc.sync.dma_start(
                out=out_0[n0:n0 + P, g * SPAN:(g + 1) * SPAN], in_=rows[:].rearrange("n m t -> n (m t)")
            )

        interleave_w_pair(0, 0, 0, on_scalar=False)
        interleave_w_pair(0, 0, 1, on_scalar=True)
        quantize_w(0, 0, 0)
        interleave_w_pair(1, 0, 0, on_scalar=False)
        interleave_w_pair(1, 0, 1, on_scalar=True)
        quantize_w(0, 0, 2)
        quantize_w(1, 0, 0)
        quantize_w(1, 0, 2)

        slots = list(range(PACK))
        multiply(0, slots, FIRST_HALF)
        tanh(0, slots, FIRST_HALF)
        scale(0, slots, FIRST_HALF)
        multiply(0, slots, SECOND_HALF)
        interleave_y(0, FIRST_HALF)
        tanh(0, slots, SECOND_HALF)
        scale(0, slots, SECOND_HALF)
        multiply(1, slots)
        quantize_y(0, FIRST_HALF)

        banks = list(range(BLOCKS))
        for s in range(STEPS - 2):
            for j in banks:
                transpose(s, j, j)
            if s == 0:
                interleave_y(0, SECOND_HALF)
                interleave_w(0, 1)
                quantize_y(0, SECOND_HALF)
            elif s == 1:
                interleave_w(1, 1)
                interleave_y(s)
            else:
                interleave_y(s)
            on_vector = banks[:1] if s >= VECTOR_COPIES_FROM else []
            for j in on_vector:
                emit(s, j, on_scalar=False)
            if s > 0:
                slots = swap_pairs(slots)
            tanh(s + 1, slots)
            scale(s + 1, last_first(slots) if s + 2 < LAST else slots)
            if s < PASSES:
                quantize_w(s, 1, 0)
            if s > 0:
                quantize_y(s)
            multiply(s + 2, slots if s + 2 < LAST else slots[:EARLY_SLOTS])
            on_scalar = banks[len(on_vector):]
            if s > 0:
                on_scalar = last_first(on_scalar)
            for j in on_scalar:
                emit(s, j, on_scalar=True)
            for part in (HALVES if s == 0 else (WHOLE,)):
                store_codes(s, part)
            if s == CHUNKS - 1:
                store_scales(0)
            banks = on_vector + on_scalar

        s = LAST - 1
        for j in banks:
            transpose(s, j, j)
        multiply(LAST, slots[EARLY_SLOTS:])
        interleave_y(s)
        for j in banks[:-1]:
            emit(s, j, on_scalar=True)
        emit(s, banks[-1], on_scalar=False)
        quantize_y(s)
        store_codes(s)

        tanh(LAST, slots, FIRST_HALF)
        scale(LAST, slots, FIRST_HALF)
        for j in range(BLOCKS // 2):
            transpose(LAST, j, banks[j])
        interleave_y(LAST, FIRST_HALF)
        tanh(LAST, slots, SECOND_HALF)
        scale(LAST, slots, SECOND_HALF)
        for j in range(BLOCKS // 2, BLOCKS):
            transpose(LAST, j, banks[j])
        quantize_y(LAST, FIRST_HALF)
        emit(LAST, 0, on_scalar=True)
        store_codes(LAST, FIRST_HALF)
        emit(LAST, 1, on_scalar=True)
        interleave_y(LAST, SECOND_HALF)
        emit(LAST, 2, on_scalar=True)
        quantize_y(LAST, SECOND_HALF)
        store_codes(LAST, SECOND_HALF)
        store_scales(GROUPS - 1)
        emit(LAST, 3, on_scalar=True)
